import numpy as np
import ml_dtypes


def mxq(x, axis, fmt="e4m3"):
    dtype, down = {"e4m3": (ml_dtypes.float8_e4m3fn, 7), "e5m2": (ml_dtypes.float8_e5m2, 14)}[fmt]
    v = np.moveaxis(np.asarray(x, np.float32).astype(ml_dtypes.bfloat16).astype(np.float64), axis, -1)
    blocks = v.reshape(v.shape[:-1] + (-1, 32))
    amax = np.abs(blocks).max(-1, keepdims=True)
    byte = np.maximum(np.where(amax > 0, np.frexp(amax)[1] - 1 + 127, 0) - down, 1)
    scale = np.exp2(byte - 127.0)
    codes = (blocks / scale).astype(np.float32).astype(dtype).astype(np.float64)
    return np.moveaxis((codes * scale).reshape(v.shape), -1, axis)


WIDE = False


def mx_kscale(k):
    if not WIDE:
        return np.ones(k)
    levels = np.array([10, -10, 5, -5, 0])
    if k % 512:
        return np.exp2(np.random.permutation(np.resize(levels, k // 32))).repeat(32)
    a = np.empty((k // 512, 16))
    for p in range(k // 512):
        a[p, :8] = np.random.permutation(np.resize(levels, 8))
        for g in range(8):
            far = levels[np.abs(levels - a[p, g]) >= 10]
            a[p, g + 8] = far[np.random.randint(len(far))]
    return np.exp2(a.ravel()).repeat(32)


def f64(x):
    return np.asarray(x).astype(np.float64)


def striped(idx):
    return np.tile(idx.reshape(-1, 16).T, (8, 1)).astype(np.uint16)


def unstriped(offs):
    return offs[:16].T.reshape(-1).astype(np.int64)


E2M1 = np.array([0.0, 0.5, 1.0, 1.5, 2.0, 3.0, 4.0, 6.0, -0.0, -0.5, -1.0, -1.5, -2.0, -3.0, -4.0, -6.0])


def pack_weight(w, fmt):
    k, n = w.shape
    w = f64(np.asarray(w, np.float32).astype(ml_dtypes.bfloat16)).reshape(k // 32, 32, n)
    amax = np.abs(w).max(1)
    if fmt == "e4m3":
        byte = np.frexp(amax)[1] - 1 + 127 - 7
    else:
        mant, ex = np.frexp(amax / 6.0)
        byte = np.where(mant > 0.5, ex, ex - 1) + 127
    byte = np.clip(np.where(amax > 0, byte, 1), 1, 254)
    scaled = (w * np.exp2(127.0 - byte)[:, None, :]).reshape(k, n).astype(np.float32)
    by_word = np.ascontiguousarray(scaled.reshape(k // 512, 128, 4, n).transpose(0, 1, 3, 2))
    if fmt == "e4m3":
        words = by_word.astype(ml_dtypes.float8_e4m3fn).view(np.uint8)
    else:
        c = by_word.astype(ml_dtypes.float4_e2m1fn).view(np.uint8) & 0xF
        words = (c[..., 0::2] | (c[..., 1::2] << 4)).reshape(k // 512, 128, 2 * n)
    return np.ascontiguousarray(words), np.ascontiguousarray(byte.astype(np.uint8).reshape(k // 512, 16, n))


def unpack_weight(words, scales, fmt):
    g, _, n = scales.shape
    words = np.ascontiguousarray(words).reshape(g, 128, n, -1)
    if fmt == "e4m3":
        vals = words.view(ml_dtypes.float8_e4m3fn).astype(np.float64)
    else:
        nib = np.empty((g, 128, n, 4), np.uint8)
        nib[..., 0::2] = words & 0xF
        nib[..., 1::2] = words >> 4
        vals = E2M1[nib]
    vals = vals * np.repeat(np.exp2(scales.astype(np.float64) - 127.0), 8, axis=1)[..., None]
    return vals.transpose(0, 1, 3, 2).reshape(g * 512, n)


def gelu(v):
    return 0.5 * v * (1.0 + np.tanh(np.sqrt(2.0 / np.pi) * (v + 0.044715 * v**3)))


K, H, N, T, S, P = 1024, 1024, 512, 2048, 1024, 512

def setup_inputs():
    n = np.random.standard_normal
    s = mx_kscale(K)[:, None]
    u = mx_kscale(H)[:, None]
    tab_words, tab_scales = pack_weight(n((K, T)) * s, "e4m3")
    w2_words, w2_scales = pack_weight(0.5 * n((K, H)) / np.sqrt(K) / s, "e2m1")
    w3_words, w3_scales = pack_weight(n((H, N)) / np.sqrt(H) / u, "e4m3")
    return {
        "tab_words": tab_words, "tab_scales": tab_scales,
        "offs": striped(np.random.permutation(T)[:S]),
        "pos1": striped(np.random.permutation(S)[:P]),
        "pos2": striped(np.random.permutation(S)[:P]),
        "w1": (1.2 * n((K, H)) / np.sqrt(K) / s).astype(np.float32),
        "w2_words": w2_words, "w2_scales": w2_scales,
        "temp": np.random.uniform(0.4, 1.6, H).astype(np.float32),
        "depth": (np.random.uniform(1.0, 5.0, (H, P)) * u).astype(np.float32),
        "w3_words": w3_words, "w3_scales": w3_scales,
        "res": (0.7 * n((N, P))).astype(np.float32),
    }

def reference(tab_words, tab_scales, offs, pos1, pos2, w1, w2_words, w2_scales,
              temp, depth, w3_words, w3_scales, res):
    v = unpack_weight(tab_words, tab_scales, "e4m3")[:, unstriped(offs)]
    w2 = unpack_weight(w2_words, w2_scales, "e2m1")
    w3 = unpack_weight(w3_words, w3_scales, "e4m3")
    f = mxq(f64(w1), 0, "e4m3").T @ v
    h = np.tanh(f) + (w2.T @ v)
    top = h.max(axis=1)
    a = np.exp(f64(temp)[:, None] * (h[:, unstriped(pos1)] - top[:, None]))
    c = f[:, unstriped(pos2)]
    y = a * c * f64(depth)
    return np.tanh((w3.T @ mxq(y, 0, "e4m3")) + f64(res))

@@ -1,0 +1,275 @@
+from contextlib import ExitStack
+
+import concourse.mybir as mybir
+
+K, H, N, T, S, M = 1024, 1024, 512, 2048, 1024, 512
+FLOPS = 2 * K * H * S * 2 + 2 * H * N * M
+
+F32 = mybir.dt.float32
+BF16 = mybir.dt.bfloat16
+I32 = mybir.dt.int32
+U32 = mybir.dt.uint32
+U16 = mybir.dt.uint16
+U8 = mybir.dt.uint8
+FP8X4 = mybir.dt.float8_e4m3fn_x4
+FP4X4 = mybir.dt.float4_e2m1fn_x4
+ALU = mybir.AluOpType
+ACT = mybir.ActivationFunctionType
+
+P = 128
+PACK = 4
+PASS = P * PACK
+BANK = 512
+LIVE = 100
+
+
+def tile_list_nodule_puncture_scores_kernel(
+    tc, tab_words, tab_scales, offs, pos1, pos2, w1, w2_words, w2_scales, temp, depth, w3_words, w3_scales, res, out
+):
+    nc = tc.nc
+    with ExitStack() as ctx:
+        keep = ctx.enter_context(tc.tile_pool(name="keep", bufs=1))
+        ring = ctx.enter_context(tc.tile_pool(name="ring", bufs=3))
+        psum = ctx.enter_context(tc.psum_pool(name="psum", bufs=8))
+
+        def held(name, shape, dtype):
+            return keep.tile(shape, dtype, name=name, align_bytes=64)
+
+        offs_sb = held("offs_sb", [P, S // 16], U16)
+        pos1_sb = held("pos1_sb", [P, M // 16], U16)
+        pos2_sb = held("pos2_sb", [P, M // 16], U16)
+        temp_sb = held("temp_sb", [P, 2, PACK], F32)
+        neg_temp = held("neg_temp", [P, 2 * PACK], F32)
+        bias = held("bias", [P, 2 * PACK], F32)
+        tab_w = [held("tab_w%d" % a, [P, T], U32) for a in range(2)]
+        tab_s = held("tab_s", [P, T], U8)
+        v_w = [[held("v_w%d%d" % (a, hf), [P, BANK], U32) for hf in range(2)] for a in range(2)]
+        v_s = held("v_s", [P, S], U8)
+        v_s1 = held("v_s1", [P, S], U8)
+        w1_raw = [[[held("w1_raw%d%d%d" % (b, a, c), [P, PACK, 256], F32) for c in range(2)] for a in range(2)] for b in range(2)]
+        w1_bf = [[held("w1_bf%d%d" % (b, a), [P, PACK, P, PACK], BF16) for a in range(2)] for b in range(2)]
+        w1_w = [[held("w1_w%d%d" % (b, a), [P, PASS], U32) for a in range(2)] for b in range(2)]
+        w1_s = [[held("w1_s%d%d" % (b, a), [P, PASS], U8) for a in range(2)] for b in range(2)]
+        w2_raw = held("w2_raw", [P, 2, H], U16)
+        w2_w = [held("w2_w%d" % b, [P, 2, PASS], U16) for b in range(2)]
+        w2_sraw = held("w2_sraw", [P, H], U8)
+        w2_s = held("w2_s", [P, H], U8)
+        w2_s1 = held("w2_s1", [P, H], U8)
+        dep = [held("dep%d" % b, [P, PACK, M], F32) for b in range(2)]
+        w3_w = held("w3_w", [P, 2, N], U32)
+        w3_s = held("w3_s", [P, N], U8)
+        res_sb = held("res_sb", [P, N // P, M], F32)
+        look = [held("look%d" % b, [P, PACK, M], F32) for b in range(2)]
+        pick = [held("pick%d" % b, [P, PACK, M], F32) for b in range(2)]
+        y_bf = [[held("y_bf%d%d" % (b, hf), [P, 256, PACK], BF16) for hf in range(2)] for b in range(2)]
+        y_w = [[held("y_w%d%d" % (b, hf), [P, 256], U32) for hf in range(2)] for b in range(2)]
+        y_s = [[held("y_s%d%d" % (b, hf), [P, 256], U8) for hf in range(2)] for b in range(2)]
+        scaled = held("scaled", [P, S], F32)
+
+        def load_scales(queue, plane, scales):
+            for q in range(4):
+                queue.dma_start(out=plane[32 * q : 32 * q + 8, :].bitcast(I32), in_=scales[:, 4 * q : 4 * q + 4, :].bitcast(I32))
+
+        def load_w1(b, a, c):
+            rows = w1[a * PASS : (a + 1) * PASS, b * PASS + c * 256 : b * PASS + (c + 1) * 256]
+            nc.sync.dma_start(out=w1_raw[b][a][c][:], in_=rows.rearrange("(p j) r -> p j r", j=PACK))
+
+        def round_w1(b, a, c):
+            nc.scalar.copy(
+                out=w1_bf[b][a][:, :, 64 * c : 64 * (c + 1), :].rearrange("p i q j -> p q j i"),
+                in_=w1_raw[b][a][c][:].rearrange("p j (q i) -> p q j i", i=PACK),
+            )
+
+        def quantize(codes, scales, values):
+            nc.vector.quantize_mx(out=codes[:].bitcast(FP8X4), scales=scales[:], in_=values)
+
+        def quantize_w1(b, a):
+            quantize(w1_w[b][a], w1_s[b][a], w1_bf[b][a][:].rearrange("p i q j -> p (i q j)"))
+
+        def load_depth(b):
+            nc.sync.dma_start(out=dep[b][:], in_=depth[b * PASS : (b + 1) * PASS, :].rearrange("(p i) m -> p i m", i=PACK))
+
+        for plane in (tab_s, v_s1, w2_s1, w3_s):
+            nc.vector.memset(plane[:].bitcast(I32), 0)
+        nc.gpsimd.memset(w2_sraw[:].bitcast(I32), 0)
+
+        nc.sync.dma_start(offs_sb[:], offs)
+        nc.sync.dma_start(pos1_sb[:], pos1)
+        nc.sync.dma_start(pos2_sb[:], pos2)
+        nc.sync.dma_start(out=temp_sb[:], in_=temp.rearrange("(b p i) -> p b i", b=2, i=PACK))
+        for a in range(2):
+            nc.sync.dma_start(out=tab_w[a][:].bitcast(I32), in_=tab_words[a].rearrange("p t i -> p (t i)").bitcast(I32))
+        load_scales(nc.scalar, tab_s, tab_scales)
+        load_scales(nc.gpsimd, w2_sraw, w2_scales)
+        for a in range(2):
+            for c in range(2):
+                load_w1(0, a, c)
+        nc.sync.dma_start(out=w2_raw[:].bitcast(I32), in_=w2_words.rearrange("a p c -> p a c").bitcast(I32))
+
+        def gather_words(a, hf):
+            nc.vector.tensor_copy(out=v_w[a][hf][:], in_=tab_w[a][:].indirect(offs_sb[:, 32 * hf : 32 * (hf + 1)]))
+
+        gather_words(0, 0)
+        gather_words(0, 1)
+        nc.vector.tensor_copy(out=v_s[:], in_=tab_s[:].indirect(offs_sb[:]))
+        nc.sync.dma_start(out=v_s1[0:LIVE, :].bitcast(I32), in_=v_s[4 : 4 + LIVE, :].bitcast(I32))
+        nc.vector.tensor_copy(
+            out=w2_s[:].rearrange("p (b i q) -> p b i q", b=2, i=PACK),
+            in_=w2_sraw[:].rearrange("p (b q i) -> p b i q", b=2, i=PACK),
+        )
+        nc.sync.dma_start(out=w2_s1[0:LIVE, :].bitcast(I32), in_=w2_s[4 : 4 + LIVE, :].bitcast(I32))
+        nc.vector.tensor_scalar(neg_temp[:], temp_sb[:].rearrange("p b i -> p (b i)"), -1.0, None, ALU.mult)
+        for a in range(2):
+            gather_words(1, a)
+            for c in range(2):
+                round_w1(0, a, c)
+            quantize_w1(0, a)
+        for b in range(2):
+            nc.vector.tensor_copy(
+                out=w2_w[b][:].rearrange("p a (i q) -> p a i q", i=PACK),
+                in_=w2_raw[:, :, b * PASS : (b + 1) * PASS].rearrange("p a (q i) -> p a i q", i=PACK),
+            )
+
+        load_depth(0)
+        for a in range(2):
+            for c in range(2):
+                load_w1(1, a, c)
+        load_depth(1)
+        nc.sync.dma_start(out=w3_w[:].bitcast(I32), in_=w3_words.rearrange("a p c i -> p a (c i)").bitcast(I32))
+        load_scales(nc.sync, w3_s, w3_scales)
+        nc.sync.dma_start(out=res_sb[:], in_=res.rearrange("(t p) m -> p t m", p=P))
+
+        f_sb, h_sb = {}, {}
+
+        def first_stage(t):
+            b, i = divmod(t, PACK)
+            cols = slice(i * P, (i + 1) * P)
+            s_cols = slice(b * PASS + i * P, b * PASS + (i + 1) * P)
+            f_ps = [psum.tile([P, BANK], F32, name="bank") for hf in range(2)]
+            g_ps = [psum.tile([P, BANK], F32, name="bank") for hf in range(2)]
+            for hf in range(2):
+                js = slice(hf * BANK, (hf + 1) * BANK)
+                for a in range(2):
+                    nc.tensor.matmul_mx(
+                        out=f_ps[hf][:],
+                        lhsT=w1_w[b][a][:, cols].bitcast(FP8X4),
+                        lhsT_scale=w1_s[b][a][:, cols],
+                        rhs=v_w[a][hf][:].bitcast(FP8X4),
+                        rhs_scale=v_s[4 * a : P, js],
+                        start=(a == 0),
+                        stop=(a == 1),
+                    )
+            for hf in range(2):
+                js = slice(hf * BANK, (hf + 1) * BANK)
+                for a in range(2):
+                    nc.tensor.matmul_mx(
+                        out=g_ps[hf][:],
+                        lhsT=w2_w[b][:, a, cols].bitcast(FP4X4),
+                        lhsT_scale=(w2_s, w2_s1)[a][:, s_cols],
+                        rhs=v_w[a][hf][:].bitcast(FP8X4),
+                        rhs_scale=(v_s, v_s1)[a][:, js],
+                        start=(a == 0),
+                        stop=(a == 1),
+                    )
+            tanh_f = ring.tile([P, S], F32, name="tanh_f", bufs=2)
+            f_sb[t] = ring.tile([P, S], F32, name="f_sb")
+            h_sb[t] = ring.tile([P, S], F32, name="h_sb")
+            for hf in range(2):
+                js = slice(hf * BANK, (hf + 1) * BANK)
+                nc.scalar.activation(out=tanh_f[:, js], in_=f_ps[hf][:], func=ACT.Tanh)
+                nc.vector.tensor_tensor(h_sb[t][:, js], g_ps[hf][:], tanh_f[:, js], ALU.add)
+            return f_ps
+
+        def keep_f(t, f_ps):
+            for hf in range(2):
+                nc.scalar.copy(out=f_sb[t][:, hf * BANK : (hf + 1) * BANK], in_=f_ps[hf][:])
+
+        def row_bias(t):
+            nc.vector.tensor_scalar(
+                scaled[:], h_sb[t][:], neg_temp[:, t : t + 1], None, ALU.mult, ALU.min, accum_out=bias[:, t : t + 1]
+            )
+
+        def pick_f(t):
+            b, i = divmod(t, PACK)
+            nc.vector.tensor_tensor(pick[b][:, i, :], f_sb[t][:].indirect(pos2_sb[:]), dep[b][:, i, :], ALU.mult)
+
+        def look_h(t, parts):
+            b, i = divmod(t, PACK)
+            width = M // parts
+            for u in range(parts):
+                nc.scalar.activation(
+                    out=look[b][:, i, u * width : (u + 1) * width],
+                    in_=h_sb[t][:].indirect(pos1_sb[:, u * width // 16 : (u + 1) * width // 16]),
+                    func=ACT.Exp,
+                    bias=bias[:, t : t + 1],
+                    scale=temp_sb[:, b, i : i + 1],
+                )
+
+        def make_y(b, hf):
+            ms = slice(hf * 256, (hf + 1) * 256)
+            nc.vector.tensor_tensor(
+                y_bf[b][hf][:].rearrange("p (c u) i -> p c i u", u=4),
+                look[b][:, :, ms].rearrange("p i (c u) -> p c i u", u=4),
+                pick[b][:, :, ms].rearrange("p i (c u) -> p c i u", u=4),
+                ALU.mult,
+            )
+
+        def quantize_y(b, hf):
+            quantize(y_w[b][hf], y_s[b][hf], y_bf[b][hf][:].rearrange("p m i -> p (m i)"))
+
+        tiles = 2 * PACK
+        for t in range(tiles):
+            f_ps = first_stage(t)
+            if t > 0:
+                look_h(t - 1, 1)
+                pick_f(t - 1)
+            keep_f(t, f_ps)
+            row_bias(t)
+            if t < 3:
+                pieces = ((0, 0),) if t == 0 else ((0, 1), (1, 0)) if t == 1 else ((1, 1),)
+                for a, c in pieces:
+                    round_w1(1, a, c)
+                    if c == 1:
+                        quantize_w1(1, a)
+            if t in (4, 5):
+                make_y(0, t - 4)
+            if t in (5, 6):
+                quantize_y(0, t - 5)
+        pick_f(tiles - 1)
+        look_h(tiles - 1, 2)
+
+        out_v = out.rearrange("(t p) m -> p t m", p=P)
+        acc = {}
+        for hf in range(2):
+            for k in range(2):
+                acc[hf, k] = psum.tile([P, 2, 256], F32, name="bank")
+
+        def second_stage(b, hf):
+            for k in range(2):
+                for u in range(2):
+                    ns = slice((2 * k + u) * P, (2 * k + u + 1) * P)
+                    nc.tensor.matmul_mx(
+                        out=acc[hf, k][:, u, :],
+                        lhsT=w3_w[:, b, ns].bitcast(FP8X4),
+                        lhsT_scale=w3_s[4 * b : P, ns],
+                        rhs=y_w[b][hf][:].bitcast(FP8X4),
+                        rhs_scale=y_s[b][hf][:],
+                        start=(b == 0 and u == 0),
+                        stop=(b == 1 and u == 1),
+                    )
+
+        for hf in range(2):
+            second_stage(0, hf)
+        for hf in range(2):
+            make_y(1, hf)
+        for hf in range(2):
+            quantize_y(1, hf)
+            second_stage(1, hf)
+        for hf in range(2):
+            ms = slice(hf * 256, (hf + 1) * 256)
+            for k in range(2):
+                total = ring.tile([P, 2, 256], F32, name="total")
+                score = ring.tile([P, 2, 256], F32, name="score", bufs=4)
+                nc.vector.tensor_tensor(total[:], acc[hf, k][:], res_sb[:, 2 * k : 2 * k + 2, ms], ALU.add)
+                nc.scalar.activation(out=score[:], in_=total[:], func=ACT.Tanh)
+                nc.sync.dma_start(out=out_v[:, 2 * k : 2 * k + 2, ms], in_=score[:])

@@ -20,7 +20,6 @@ P = 128
 PACK = 4
 PASS = P * PACK
 BANK = 512
-LIVE = 100
 
 
 def tile_list_nodule_puncture_scores_kernel(
@@ -30,7 +29,7 @@ def tile_list_nodule_puncture_scores_kernel(
     with ExitStack() as ctx:
         keep = ctx.enter_context(tc.tile_pool(name="keep", bufs=1))
         ring = ctx.enter_context(tc.tile_pool(name="ring", bufs=3))
-        psum = ctx.enter_context(tc.psum_pool(name="psum", bufs=8))
+        psum = ctx.enter_context(tc.psum_pool(name="psum", bufs=4))
 
         def held(name, shape, dtype):
             return keep.tile(shape, dtype, name=name, align_bytes=64)
@@ -45,16 +44,15 @@ def tile_list_nodule_puncture_scores_kernel(
         tab_s = held("tab_s", [P, T], U8)
         v_w = [[held("v_w%d%d" % (a, hf), [P, BANK], U32) for hf in range(2)] for a in range(2)]
         v_s = held("v_s", [P, S], U8)
-        v_s1 = held("v_s1", [P, S], U8)
+        v_s0 = [held("v_s0%d" % a, [P, S], U8) for a in range(2)]
         w1_raw = [[[held("w1_raw%d%d%d" % (b, a, c), [P, PACK, 256], F32) for c in range(2)] for a in range(2)] for b in range(2)]
         w1_bf = [[held("w1_bf%d%d" % (b, a), [P, PACK, P, PACK], BF16) for a in range(2)] for b in range(2)]
         w1_w = [[held("w1_w%d%d" % (b, a), [P, PASS], U32) for a in range(2)] for b in range(2)]
         w1_s = [[held("w1_s%d%d" % (b, a), [P, PASS], U8) for a in range(2)] for b in range(2)]
-        w2_raw = held("w2_raw", [P, 2, H], U16)
+        w2_raw = [held("w2_raw%d" % b, [P, 2, PASS], U16) for b in range(2)]
         w2_w = [held("w2_w%d" % b, [P, 2, PASS], U16) for b in range(2)]
-        w2_sraw = held("w2_sraw", [P, H], U8)
-        w2_s = held("w2_s", [P, H], U8)
-        w2_s1 = held("w2_s1", [P, H], U8)
+        w2_sraw = held("w2_sraw", [P, 2, H], U8)
+        w2_s = [held("w2_s%d" % b, [P, 2, PASS], U8) for b in range(2)]
         dep = [held("dep%d" % b, [P, PACK, M], F32) for b in range(2)]
         w3_w = held("w3_w", [P, 2, N], U32)
         w3_s = held("w3_s", [P, N], U8)
@@ -66,87 +64,115 @@ def tile_list_nodule_puncture_scores_kernel(
         y_s = [[held("y_s%d%d" % (b, hf), [P, 256], U8) for hf in range(2)] for b in range(2)]
         scaled = held("scaled", [P, S], F32)
 
-        def load_scales(queue, plane, scales):
+        def load_scales(queue, plane, scales, first):
             for q in range(4):
-                queue.dma_start(out=plane[32 * q : 32 * q + 8, :].bitcast(I32), in_=scales[:, 4 * q : 4 * q + 4, :].bitcast(I32))
+                rows = slice(32 * q + first, 32 * q + first + 8)
+                queue.dma_start(out=plane[rows, :].bitcast(I32), in_=scales[:, 4 * q : 4 * q + 4, :].bitcast(I32))
 
         def load_w1(b, a, c):
             rows = w1[a * PASS : (a + 1) * PASS, b * PASS + c * 256 : b * PASS + (c + 1) * 256]
             nc.sync.dma_start(out=w1_raw[b][a][c][:], in_=rows.rearrange("(p j) r -> p j r", j=PACK))
 
-        def round_w1(b, a, c):
-            nc.scalar.copy(
+        def round_w1(b, a, c, copy=nc.scalar.copy):
+            copy(
                 out=w1_bf[b][a][:, :, 64 * c : 64 * (c + 1), :].rearrange("p i q j -> p q j i"),
                 in_=w1_raw[b][a][c][:].rearrange("p j (q i) -> p q j i", i=PACK),
             )
 
         def quantize(codes, scales, values):
-            nc.vector.quantize_mx(out=codes[:].bitcast(FP8X4), scales=scales[:], in_=values)
+            nc.vector.quantize_mx(out=codes.bitcast(FP8X4), scales=scales, in_=values)
 
-        def quantize_w1(b, a):
-            quantize(w1_w[b][a], w1_s[b][a], w1_bf[b][a][:].rearrange("p i q j -> p (i q j)"))
+        def quantize_w1(b, a, i0=0, i1=PACK):
+            cols = slice(i0 * P, i1 * P)
+            quantize(w1_w[b][a][:, cols], w1_s[b][a][:, cols], w1_bf[b][a][:, i0:i1, :, :].rearrange("p i q j -> p (i q j)"))
 
         def load_depth(b):
             nc.sync.dma_start(out=dep[b][:], in_=depth[b * PASS : (b + 1) * PASS, :].rearrange("(p i) m -> p i m", i=PACK))
 
-        for plane in (tab_s, v_s1, w2_s1, w3_s):
-            nc.vector.memset(plane[:].bitcast(I32), 0)
+        for q in range(4):
+            nc.vector.memset(tab_s[32 * q : 32 * q + 24, :].bitcast(I32), 0)
+        for a in range(2):
+            nc.gpsimd.memset(v_s0[a][96:P, :].bitcast(I32), 0)
         nc.gpsimd.memset(w2_sraw[:].bitcast(I32), 0)
+        nc.gpsimd.memset(w3_s[:].bitcast(I32), 0)
 
         nc.sync.dma_start(offs_sb[:], offs)
-        nc.sync.dma_start(pos1_sb[:], pos1)
-        nc.sync.dma_start(pos2_sb[:], pos2)
-        nc.sync.dma_start(out=temp_sb[:], in_=temp.rearrange("(b p i) -> p b i", b=2, i=PACK))
-        for a in range(2):
+        load_scales(nc.sync, tab_s, tab_scales, 24)
+
+        def load_table(a):
             nc.sync.dma_start(out=tab_w[a][:].bitcast(I32), in_=tab_words[a].rearrange("p t i -> p (t i)").bitcast(I32))
-        load_scales(nc.scalar, tab_s, tab_scales)
-        load_scales(nc.gpsimd, w2_sraw, w2_scales)
-        for a in range(2):
-            for c in range(2):
-                load_w1(0, a, c)
-        nc.sync.dma_start(out=w2_raw[:].bitcast(I32), in_=w2_words.rearrange("a p c -> p a c").bitcast(I32))
+
+        def load_w2(b):
+            words = w2_words[:, :, 2 * b * PASS : 2 * (b + 1) * PASS]
+            nc.sync.dma_start(out=w2_raw[b][:].bitcast(I32), in_=words.rearrange("a p c -> p a c").bitcast(I32))
+
+        def shift_scales(a, rows):
+            nc.sync.dma_start(out=v_s0[a][0:rows, :].bitcast(I32), in_=v_s[P - rows : P, :].bitcast(I32))
 
         def gather_words(a, hf):
             nc.vector.tensor_copy(out=v_w[a][hf][:], in_=tab_w[a][:].indirect(offs_sb[:, 32 * hf : 32 * (hf + 1)]))
 
-        gather_words(0, 0)
-        gather_words(0, 1)
-        nc.vector.tensor_copy(out=v_s[:], in_=tab_s[:].indirect(offs_sb[:]))
-        nc.sync.dma_start(out=v_s1[0:LIVE, :].bitcast(I32), in_=v_s[4 : 4 + LIVE, :].bitcast(I32))
-        nc.vector.tensor_copy(
-            out=w2_s[:].rearrange("p (b i q) -> p b i q", b=2, i=PACK),
-            in_=w2_sraw[:].rearrange("p (b q i) -> p b i q", b=2, i=PACK),
-        )
-        nc.sync.dma_start(out=w2_s1[0:LIVE, :].bitcast(I32), in_=w2_s[4 : 4 + LIVE, :].bitcast(I32))
-        nc.vector.tensor_scalar(neg_temp[:], temp_sb[:].rearrange("p b i -> p (b i)"), -1.0, None, ALU.mult)
-        for a in range(2):
-            gather_words(1, a)
-            for c in range(2):
-                round_w1(0, a, c)
-            quantize_w1(0, a)
-        for b in range(2):
-            nc.vector.tensor_copy(
-                out=w2_w[b][:].rearrange("p a (i q) -> p a i q", i=PACK),
-                in_=w2_raw[:, :, b * PASS : (b + 1) * PASS].rearrange("p a (q i) -> p a i q", i=PACK),
-            )
+        def deal_w2(b):
+            for copy, dealt, raw in (
+                (nc.vector.tensor_copy, w2_s, w2_sraw[:, :, b * PASS : (b + 1) * PASS]),
+                (nc.scalar.copy, w2_w, w2_raw[b][:]),
+            ):
+                copy(
+                    out=dealt[b][:].rearrange("p a (i q) -> p a i q", i=PACK),
+                    in_=raw.rearrange("p a (q i) -> p a i q", i=PACK),
+                )
 
+        load_table(0)
+        load_w2(0)
+        load_w1(0, 0, 0)
+        for q in range(4):
+            nc.sync.dma_start(
+                out=w2_sraw[32 * q : 32 * q + 4, :, :].bitcast(I32),
+                in_=w2_scales[:, 4 * q : 4 * q + 4, :].rearrange("a r c -> r a c").bitcast(I32),
+            )
+        load_table(1)
+        nc.vector.tensor_copy(out=v_s[:], in_=tab_s[:].indirect(offs_sb[:]))
+        shift_scales(0, 104)
+        shift_scales(1, 100)
+        load_w1(0, 0, 1)
+        load_w1(0, 1, 0)
+        load_w1(0, 1, 1)
+        load_w2(1)
+        nc.sync.dma_start(out=temp_sb[:], in_=temp.rearrange("(b p i) -> p b i", b=2, i=PACK))
+        nc.sync.dma_start(pos1_sb[:], pos1)
+        nc.sync.dma_start(pos2_sb[:], pos2)
         load_depth(0)
-        for a in range(2):
-            for c in range(2):
-                load_w1(1, a, c)
+        load_w1(1, 0, 0)
+        load_w1(1, 0, 1)
+        load_w1(1, 1, 0)
+        load_w1(1, 1, 1)
         load_depth(1)
         nc.sync.dma_start(out=w3_w[:].bitcast(I32), in_=w3_words.rearrange("a p c i -> p a (c i)").bitcast(I32))
-        load_scales(nc.sync, w3_s, w3_scales)
+        load_scales(nc.sync, w3_s, w3_scales, 0)
         nc.sync.dma_start(out=res_sb[:], in_=res.rearrange("(t p) m -> p t m", p=P))
+
+        gather_words(0, 0)
+        gather_words(0, 1)
+        deal_w2(0)
+        gather_words(1, 0)
+        gather_words(1, 1)
+        round_w1(0, 0, 0)
+        round_w1(0, 0, 1)
+        quantize_w1(0, 0)
+        round_w1(0, 1, 0)
+        round_w1(0, 1, 1, nc.vector.tensor_copy)
+        quantize_w1(0, 1, 0, 1)
+        quantize_w1(0, 1, 1, PACK)
+        nc.vector.tensor_scalar(neg_temp[:], temp_sb[:].rearrange("p b i -> p (b i)"), -1.0, None, ALU.mult)
+        deal_w2(1)
 
         f_sb, h_sb = {}, {}
 
         def first_stage(t):
             b, i = divmod(t, PACK)
             cols = slice(i * P, (i + 1) * P)
-            s_cols = slice(b * PASS + i * P, b * PASS + (i + 1) * P)
-            f_ps = [psum.tile([P, BANK], F32, name="bank") for hf in range(2)]
-            g_ps = [psum.tile([P, BANK], F32, name="bank") for hf in range(2)]
+            f_ps = [psum.tile([P, BANK], F32, name="f_bank") for hf in range(2)]
+            g_ps = [psum.tile([P, BANK], F32, name="g_bank", bufs=2) for hf in range(2)]
             for hf in range(2):
                 js = slice(hf * BANK, (hf + 1) * BANK)
                 for a in range(2):
@@ -155,7 +181,7 @@ def tile_list_nodule_puncture_scores_kernel(
                         lhsT=w1_w[b][a][:, cols].bitcast(FP8X4),
                         lhsT_scale=w1_s[b][a][:, cols],
                         rhs=v_w[a][hf][:].bitcast(FP8X4),
-                        rhs_scale=v_s[4 * a : P, js],
+                        rhs_scale=v_s0[0][4 * a : P, js],
                         start=(a == 0),
                         stop=(a == 1),
                     )
@@ -165,9 +191,9 @@ def tile_list_nodule_puncture_scores_kernel(
                     nc.tensor.matmul_mx(
                         out=g_ps[hf][:],
                         lhsT=w2_w[b][:, a, cols].bitcast(FP4X4),
-                        lhsT_scale=(w2_s, w2_s1)[a][:, s_cols],
+                        lhsT_scale=w2_s[b][:, a, cols],
                         rhs=v_w[a][hf][:].bitcast(FP8X4),
-                        rhs_scale=(v_s, v_s1)[a][:, js],
+                        rhs_scale=v_s0[a][:, js],
                         start=(a == 0),
                         stop=(a == 1),
                     )
@@ -189,9 +215,13 @@ def tile_list_nodule_puncture_scores_kernel(
                 scaled[:], h_sb[t][:], neg_temp[:, t : t + 1], None, ALU.mult, ALU.min, accum_out=bias[:, t : t + 1]
             )
 
-        def pick_f(t):
+        def pick_f(t, parts, factor):
             b, i = divmod(t, PACK)
-            nc.vector.tensor_tensor(pick[b][:, i, :], f_sb[t][:].indirect(pos2_sb[:]), dep[b][:, i, :], ALU.mult)
+            width = M // parts
+            for u in range(parts):
+                ms = slice(u * width, (u + 1) * width)
+                picked = f_sb[t][:].indirect(pos2_sb[:, u * width // 16 : (u + 1) * width // 16])
+                nc.vector.tensor_tensor(pick[b][:, i, ms], picked, factor[b][:, i, ms], ALU.mult)
 
         def look_h(t, parts):
             b, i = divmod(t, PACK)
@@ -205,44 +235,41 @@ def tile_list_nodule_puncture_scores_kernel(
                     scale=temp_sb[:, b, i : i + 1],
                 )
 
-        def make_y(b, hf):
-            ms = slice(hf * 256, (hf + 1) * 256)
-            nc.vector.tensor_tensor(
-                y_bf[b][hf][:].rearrange("p (c u) i -> p c i u", u=4),
-                look[b][:, :, ms].rearrange("p i (c u) -> p c i u", u=4),
-                pick[b][:, :, ms].rearrange("p i (c u) -> p c i u", u=4),
-                ALU.mult,
-            )
+        def make_y(t, factor):
+            b, i = divmod(t, PACK)
+            for hf in range(2):
+                ms = slice(hf * 256, (hf + 1) * 256)
+                nc.gpsimd.tensor_tensor(y_bf[b][hf][:, :, i], pick[b][:, i, ms], factor[b][:, i, ms], ALU.mult)
 
         def quantize_y(b, hf):
-            quantize(y_w[b][hf], y_s[b][hf], y_bf[b][hf][:].rearrange("p m i -> p (m i)"))
+            quantize(y_w[b][hf][:], y_s[b][hf][:], y_bf[b][hf][:].rearrange("p m i -> p (m i)"))
 
         tiles = 2 * PACK
+        rounders = (nc.vector.tensor_copy, nc.scalar.copy, nc.scalar.copy, nc.scalar.copy)
         for t in range(tiles):
             f_ps = first_stage(t)
             if t > 0:
                 look_h(t - 1, 1)
-                pick_f(t - 1)
+                pick_f(t - 1, 1, dep)
+                make_y(t - 1, look)
             keep_f(t, f_ps)
             row_bias(t)
-            if t < 3:
-                pieces = ((0, 0),) if t == 0 else ((0, 1), (1, 0)) if t == 1 else ((1, 1),)
-                for a, c in pieces:
-                    round_w1(1, a, c)
-                    if c == 1:
-                        quantize_w1(1, a)
-            if t in (4, 5):
-                make_y(0, t - 4)
+            for n in {0:(0,1),1:(2,),2:(3,)}.get(t, ()):
+                a, c = divmod(n, 2)
+                round_w1(1, a, c, rounders[n])
+                if c == 1:
+                    quantize_w1(1, a)
             if t in (5, 6):
                 quantize_y(0, t - 5)
-        pick_f(tiles - 1)
+        pick_f(tiles - 1, 2, dep)
         look_h(tiles - 1, 2)
+        make_y(tiles - 1, look)
 
         out_v = out.rearrange("(t p) m -> p t m", p=P)
         acc = {}
         for hf in range(2):
             for k in range(2):
-                acc[hf, k] = psum.tile([P, 2, 256], F32, name="bank")
+                acc[hf, k] = psum.tile([P, 2, 256], F32, name=("acc_bank", "f_bank")[hf], bufs=(2, 4)[hf])
 
         def second_stage(b, hf):
             for k in range(2):
@@ -260,8 +287,6 @@ def tile_list_nodule_puncture_scores_kernel(
 
         for hf in range(2):
             second_stage(0, hf)
-        for hf in range(2):
-            make_y(1, hf)
         for hf in range(2):
             quantize_y(1, hf)
             second_stage(1, hf)

@@ -45,7 +45,7 @@ def tile_list_nodule_puncture_scores_kernel(
         v_w = [[held("v_w%d%d" % (a, hf), [P, BANK], U32) for hf in range(2)] for a in range(2)]
         v_s = held("v_s", [P, S], U8)
         v_s0 = [held("v_s0%d" % a, [P, S], U8) for a in range(2)]
-        w1_raw = [[[held("w1_raw%d%d%d" % (b, a, c), [P, PACK, 256], F32) for c in range(2)] for a in range(2)] for b in range(2)]
+        w1_raw = [[held("w1_raw%d%d" % (b, a), [P, PACK, PASS], F32) for a in range(2)] for b in range(2)]
         w1_bf = [[held("w1_bf%d%d" % (b, a), [P, PACK, P, PACK], BF16) for a in range(2)] for b in range(2)]
         w1_w = [[held("w1_w%d%d" % (b, a), [P, PASS], U32) for a in range(2)] for b in range(2)]
         w1_s = [[held("w1_s%d%d" % (b, a), [P, PASS], U8) for a in range(2)] for b in range(2)]
@@ -69,14 +69,14 @@ def tile_list_nodule_puncture_scores_kernel(
                 rows = slice(32 * q + first, 32 * q + first + 8)
                 queue.dma_start(out=plane[rows, :].bitcast(I32), in_=scales[:, 4 * q : 4 * q + 4, :].bitcast(I32))
 
-        def load_w1(b, a, c):
-            rows = w1[a * PASS : (a + 1) * PASS, b * PASS + c * 256 : b * PASS + (c + 1) * 256]
-            nc.sync.dma_start(out=w1_raw[b][a][c][:], in_=rows.rearrange("(p j) r -> p j r", j=PACK))
+        def load_w1(b, a):
+            rows = w1[a * PASS : (a + 1) * PASS, b * PASS : (b + 1) * PASS]
+            nc.sync.dma_start(out=w1_raw[b][a][:], in_=rows.rearrange("(p j) r -> p j r", j=PACK))
 
-        def round_w1(b, a, c, copy=nc.scalar.copy):
+        def round_w1(copy, b, a, u):
             copy(
-                out=w1_bf[b][a][:, :, 64 * c : 64 * (c + 1), :].rearrange("p i q j -> p q j i"),
-                in_=w1_raw[b][a][c][:].rearrange("p j (q i) -> p q j i", i=PACK),
+                out=w1_bf[b][a][:, 2 * u : 2 * u + 2, :, :].rearrange("p i q j -> p q j i"),
+                in_=w1_raw[b][a][:].rearrange("p j (q i) -> p q j i", i=PACK)[:, :, :, 2 * u : 2 * u + 2],
             )
 
         def quantize(codes, scales, values):
@@ -124,28 +124,24 @@ def tile_list_nodule_puncture_scores_kernel(
 
         load_table(0)
         load_w2(0)
-        load_w1(0, 0, 0)
+        load_table(1)
         for q in range(4):
             nc.sync.dma_start(
                 out=w2_sraw[32 * q : 32 * q + 4, :, :].bitcast(I32),
                 in_=w2_scales[:, 4 * q : 4 * q + 4, :].rearrange("a r c -> r a c").bitcast(I32),
             )
-        load_table(1)
+        load_w1(0, 0)
         nc.vector.tensor_copy(out=v_s[:], in_=tab_s[:].indirect(offs_sb[:]))
         shift_scales(0, 104)
+        load_w1(0, 1)
         shift_scales(1, 100)
-        load_w1(0, 0, 1)
-        load_w1(0, 1, 0)
-        load_w1(0, 1, 1)
         load_w2(1)
         nc.sync.dma_start(out=temp_sb[:], in_=temp.rearrange("(b p i) -> p b i", b=2, i=PACK))
         nc.sync.dma_start(pos1_sb[:], pos1)
         nc.sync.dma_start(pos2_sb[:], pos2)
         load_depth(0)
-        load_w1(1, 0, 0)
-        load_w1(1, 0, 1)
-        load_w1(1, 1, 0)
-        load_w1(1, 1, 1)
+        load_w1(1, 0)
+        load_w1(1, 1)
         load_depth(1)
         nc.sync.dma_start(out=w3_w[:].bitcast(I32), in_=w3_words.rearrange("a p c i -> p a (c i)").bitcast(I32))
         load_scales(nc.sync, w3_s, w3_scales, 0)
@@ -154,15 +150,16 @@ def tile_list_nodule_puncture_scores_kernel(
         gather_words(0, 0)
         gather_words(0, 1)
         deal_w2(0)
+        round_w1(nc.scalar.copy, 0, 0, 0)
+        round_w1(nc.scalar.copy, 0, 0, 1)
         gather_words(1, 0)
         gather_words(1, 1)
-        round_w1(0, 0, 0)
-        round_w1(0, 0, 1)
-        quantize_w1(0, 0)
-        round_w1(0, 1, 0)
-        round_w1(0, 1, 1, nc.vector.tensor_copy)
-        quantize_w1(0, 1, 0, 1)
-        quantize_w1(0, 1, 1, PACK)
+        quantize_w1(0, 0, 0, 2)
+        quantize_w1(0, 0, 2, PACK)
+        round_w1(nc.vector.tensor_copy, 0, 1, 0)
+        round_w1(nc.scalar.copy, 0, 1, 1)
+        quantize_w1(0, 1, 0, 2)
+        quantize_w1(0, 1, 2, PACK)
         nc.vector.tensor_scalar(neg_temp[:], temp_sb[:].rearrange("p b i -> p (b i)"), -1.0, None, ALU.mult)
         deal_w2(1)
 
@@ -254,9 +251,9 @@ def tile_list_nodule_puncture_scores_kernel(
                 make_y(t - 1, look)
             keep_f(t, f_ps)
             row_bias(t)
-            for n in {0:(0,1),1:(2,),2:(3,)}.get(t, ()):
+            for n in {0:(0,),1:(1,),2:(2,3,)}.get(t, ()):
                 a, c = divmod(n, 2)
-                round_w1(1, a, c, rounders[n])
+                round_w1(rounders[n], 1, a, c)
                 if c == 1:
                     quantize_w1(1, a)
             if t in (5, 6):
@@ -293,8 +290,12 @@ def tile_list_nodule_puncture_scores_kernel(
         for hf in range(2):
             ms = slice(hf * 256, (hf + 1) * 256)
             for k in range(2):
-                total = ring.tile([P, 2, 256], F32, name="total")
-                score = ring.tile([P, 2, 256], F32, name="score", bufs=4)
-                nc.vector.tensor_tensor(total[:], acc[hf, k][:], res_sb[:, 2 * k : 2 * k + 2, ms], ALU.add)
-                nc.scalar.activation(out=score[:], in_=total[:], func=ACT.Tanh)
-                nc.sync.dma_start(out=out_v[:, 2 * k : 2 * k + 2, ms], in_=score[:])
+                parts = 2 if (hf, k) == (1, 1) else 1
+                for u in range(parts):
+                    us = slice(u * 2 // parts, (u + 1) * 2 // parts)
+                    ns = slice(2 * k + us.start, 2 * k + us.stop)
+                    total = ring.tile([P, 2 // parts, 256], F32, name="total")
+                    score = ring.tile([P, 2 // parts, 256], F32, name="score", bufs=5)
+                    nc.vector.tensor_tensor(total[:], acc[hf, k][:, us, :], res_sb[:, ns, ms], ALU.add)
+                    nc.scalar.activation(out=score[:], in_=total[:], func=ACT.Tanh)
+                    nc.sync.dma_start(out=out_v[:, ns, ms], in_=score[:])

@@ -59,9 +59,10 @@ def tile_list_nodule_puncture_scores_kernel(
         res_sb = held("res_sb", [P, N // P, M], F32)
         look = [held("look%d" % b, [P, PACK, M], F32) for b in range(2)]
         pick = [held("pick%d" % b, [P, PACK, M], F32) for b in range(2)]
-        y_bf = [[held("y_bf%d%d" % (b, hf), [P, 256, PACK], BF16) for hf in range(2)] for b in range(2)]
-        y_w = [[held("y_w%d%d" % (b, hf), [P, 256], U32) for hf in range(2)] for b in range(2)]
-        y_s = [[held("y_s%d%d" % (b, hf), [P, 256], U8) for hf in range(2)] for b in range(2)]
+        y_bf = [held("y_bf%d" % b, [P, M, PACK], BF16) for b in range(2)]
+        y_two = [held("y_two%d" % b, [P, 2, M, 2], BF16) for b in range(2)]
+        y_w = [held("y_w%d" % b, [P, M], U32) for b in range(2)]
+        y_s = [held("y_s%d" % b, [P, M], U8) for b in range(2)]
         scaled = held("scaled", [P, S], F32)
 
         def load_scales(queue, plane, scales, first):
@@ -232,14 +233,27 @@ def tile_list_nodule_puncture_scores_kernel(
                     scale=temp_sb[:, b, i : i + 1],
                 )
 
-        def make_y(t, factor):
+        def make_y(t):
             b, i = divmod(t, PACK)
-            for hf in range(2):
-                ms = slice(hf * 256, (hf + 1) * 256)
-                nc.gpsimd.tensor_tensor(y_bf[b][hf][:, :, i], pick[b][:, i, ms], factor[b][:, i, ms], ALU.mult)
+            for u in range(M // 256):
+                ms = slice(u * 256, (u + 1) * 256)
+                nc.gpsimd.tensor_tensor(y_two[b][:, i // 2, ms, i % 2], pick[b][:, i, ms], look[b][:, i, ms], ALU.mult)
 
-        def quantize_y(b, hf):
-            quantize(y_w[b][hf][:], y_s[b][hf][:], y_bf[b][hf][:].rearrange("p m i -> p (m i)"))
+        def make_last_y(hf):
+            ms = slice(hf * 256, (hf + 1) * 256)
+            nc.vector.tensor_tensor(
+                y_two[1][:, 1, ms, :].rearrange("p (c u) i -> p c i u", u=4),
+                pick[1][:, 2:4, ms].rearrange("p i (c u) -> p c i u", u=4),
+                look[1][:, 2:4, ms].rearrange("p i (c u) -> p c i u", u=4),
+                ALU.mult,
+            )
+
+        def quantize_y(b, ms):
+            nc.scalar.copy(
+                out=y_bf[b][:, ms, :].rearrange("p m i -> p (m i)").bitcast(F32).rearrange("p (m u) -> p m u", u=2),
+                in_=y_two[b][:, :, ms, :].rearrange("p u m l -> p u (m l)").bitcast(F32).rearrange("p u m -> p m u"),
+            )
+            quantize(y_w[b][:, ms], y_s[b][:, ms], y_bf[b][:, ms, :].rearrange("p m i -> p (m i)"))
 
         tiles = 2 * PACK
         rounders = (nc.vector.tensor_copy, nc.scalar.copy, nc.scalar.copy, nc.scalar.copy)
@@ -248,7 +262,8 @@ def tile_list_nodule_puncture_scores_kernel(
             if t > 0:
                 look_h(t - 1, 1)
                 pick_f(t - 1, 1, dep)
-                make_y(t - 1, look)
+                if t < tiles - 1:
+                    make_y(t - 1)
             keep_f(t, f_ps)
             row_bias(t)
             for n in {0:(0,),1:(1,),2:(2,3,)}.get(t, ()):
@@ -256,11 +271,10 @@ def tile_list_nodule_puncture_scores_kernel(
                 round_w1(rounders[n], 1, a, c)
                 if c == 1:
                     quantize_w1(1, a)
-            if t in (5, 6):
-                quantize_y(0, t - 5)
+            if t == 5:
+                quantize_y(0, slice(0, M))
         pick_f(tiles - 1, 2, dep)
         look_h(tiles - 1, 2)
-        make_y(tiles - 1, look)
 
         out_v = out.rearrange("(t p) m -> p t m", p=P)
         acc = {}
@@ -276,8 +290,8 @@ def tile_list_nodule_puncture_scores_kernel(
                         out=acc[hf, k][:, u, :],
                         lhsT=w3_w[:, b, ns].bitcast(FP8X4),
                         lhsT_scale=w3_s[4 * b : P, ns],
-                        rhs=y_w[b][hf][:].bitcast(FP8X4),
-                        rhs_scale=y_s[b][hf][:],
+                        rhs=y_w[b][:, hf * 256 : (hf + 1) * 256].bitcast(FP8X4),
+                        rhs_scale=y_s[b][:, hf * 256 : (hf + 1) * 256],
                         start=(b == 0 and u == 0),
                         stop=(b == 1 and u == 1),
                     )
@@ -285,7 +299,8 @@ def tile_list_nodule_puncture_scores_kernel(
         for hf in range(2):
             second_stage(0, hf)
         for hf in range(2):
-            quantize_y(1, hf)
+            make_last_y(hf)
+            quantize_y(1, slice(hf * 256, (hf + 1) * 256))
             second_stage(1, hf)
         for hf in range(2):
             ms = slice(hf * 256, (hf + 1) * 256)

from contextlib import ExitStack

import concourse.mybir as mybir

K, H, N, T, S, M = 1024, 1024, 512, 2048, 1024, 512
FLOPS = 2 * K * H * S * 2 + 2 * H * N * M

F32 = mybir.dt.float32
BF16 = mybir.dt.bfloat16
I32 = mybir.dt.int32
U32 = mybir.dt.uint32
U16 = mybir.dt.uint16
U8 = mybir.dt.uint8
FP8X4 = mybir.dt.float8_e4m3fn_x4
FP4X4 = mybir.dt.float4_e2m1fn_x4
ALU = mybir.AluOpType
ACT = mybir.ActivationFunctionType

P = 128
PACK = 4
PASS = P * PACK
BANK = 512


def tile_list_nodule_puncture_scores_kernel(
    tc, tab_words, tab_scales, offs, pos1, pos2, w1, w2_words, w2_scales, temp, depth, w3_words, w3_scales, res, out
):
    nc = tc.nc
    with ExitStack() as ctx:
        keep = ctx.enter_context(tc.tile_pool(name="keep", bufs=1))
        ring = ctx.enter_context(tc.tile_pool(name="ring", bufs=3))
        psum = ctx.enter_context(tc.psum_pool(name="psum", bufs=4))

        def held(name, shape, dtype):
            return keep.tile(shape, dtype, name=name, align_bytes=64)

        offs_sb = held("offs_sb", [P, S // 16], U16)
        pos1_sb = held("pos1_sb", [P, M // 16], U16)
        pos2_sb = held("pos2_sb", [P, M // 16], U16)
        temp_sb = held("temp_sb", [P, 2, PACK], F32)
        neg_temp = held("neg_temp", [P, 2 * PACK], F32)
        bias = held("bias", [P, 2 * PACK], F32)
        tab_w = [held("tab_w%d" % a, [P, T], U32) for a in range(2)]
        tab_s = held("tab_s", [P, T], U8)
        v_w = [[held("v_w%d%d" % (a, hf), [P, BANK], U32) for hf in range(2)] for a in range(2)]
        v_s = held("v_s", [P, S], U8)
        v_s0 = [held("v_s0%d" % a, [P, S], U8) for a in range(2)]
        w1_raw = [[held("w1_raw%d%d" % (b, a), [P, PACK, PASS], F32) for a in range(2)] for b in range(2)]
        w1_bf = [[held("w1_bf%d%d" % (b, a), [P, PACK, P, PACK], BF16) for a in range(2)] for b in range(2)]
        w1_w = [[held("w1_w%d%d" % (b, a), [P, PASS], U32) for a in range(2)] for b in range(2)]
        w1_s = [[held("w1_s%d%d" % (b, a), [P, PASS], U8) for a in range(2)] for b in range(2)]
        w2_raw = [held("w2_raw%d" % b, [P, 2, PASS], U16) for b in range(2)]
        w2_w = [held("w2_w%d" % b, [P, 2, PASS], U16) for b in range(2)]
        w2_sraw = held("w2_sraw", [P, 2, H], U8)
        w2_s = [held("w2_s%d" % b, [P, 2, PASS], U8) for b in range(2)]
        dep = [held("dep%d" % b, [P, PACK, M], F32) for b in range(2)]
        w3_w = held("w3_w", [P, 2, N], U32)
        w3_s = held("w3_s", [P, N], U8)
        res_sb = held("res_sb", [P, N // P, M], F32)
        look = [held("look%d" % b, [P, PACK, M], F32) for b in range(2)]
        pick = [held("pick%d" % b, [P, PACK, M], F32) for b in range(2)]
        y_bf = [held("y_bf%d" % b, [P, M, PACK], BF16) for b in range(2)]
        y_two = [held("y_two%d" % b, [P, 2, M, 2], BF16) for b in range(2)]
        y_w = [held("y_w%d" % b, [P, M], U32) for b in range(2)]
        y_s = [held("y_s%d" % b, [P, M], U8) for b in range(2)]
        scaled = held("scaled", [P, S], F32)

        def load_scales(queue, plane, scales, first):
            for q in range(4):
                rows = slice(32 * q + first, 32 * q + first + 8)
                queue.dma_start(out=plane[rows, :].bitcast(I32), in_=scales[:, 4 * q : 4 * q + 4, :].bitcast(I32))

        def load_w1(b, a):
            rows = w1[a * PASS : (a + 1) * PASS, b * PASS : (b + 1) * PASS]
            nc.sync.dma_start(out=w1_raw[b][a][:], in_=rows.rearrange("(p j) r -> p j r", j=PACK))

        def round_w1(copy, b, a, u):
            copy(
                out=w1_bf[b][a][:, 2 * u : 2 * u + 2, :, :].rearrange("p i q j -> p q j i"),
                in_=w1_raw[b][a][:].rearrange("p j (q i) -> p q j i", i=PACK)[:, :, :, 2 * u : 2 * u + 2],
            )

        def quantize(codes, scales, values):
            nc.vector.quantize_mx(out=codes.bitcast(FP8X4), scales=scales, in_=values)

        def quantize_w1(b, a, i0=0, i1=PACK):
            cols = slice(i0 * P, i1 * P)
            quantize(w1_w[b][a][:, cols], w1_s[b][a][:, cols], w1_bf[b][a][:, i0:i1, :, :].rearrange("p i q j -> p (i q j)"))

        def load_depth(b):
            nc.sync.dma_start(out=dep[b][:], in_=depth[b * PASS : (b + 1) * PASS, :].rearrange("(p i) m -> p i m", i=PACK))

        for q in range(4):
            nc.vector.memset(tab_s[32 * q : 32 * q + 24, :].bitcast(I32), 0)
        for a in range(2):
            nc.gpsimd.memset(v_s0[a][96:P, :].bitcast(I32), 0)
        nc.gpsimd.memset(w2_sraw[:].bitcast(I32), 0)
        nc.gpsimd.memset(w3_s[:].bitcast(I32), 0)

        nc.sync.dma_start(offs_sb[:], offs)
        load_scales(nc.sync, tab_s, tab_scales, 24)

        def load_table(a):
            nc.sync.dma_start(out=tab_w[a][:].bitcast(I32), in_=tab_words[a].rearrange("p t i -> p (t i)").bitcast(I32))

        def load_w2(b):
            words = w2_words[:, :, 2 * b * PASS : 2 * (b + 1) * PASS]
            nc.sync.dma_start(out=w2_raw[b][:].bitcast(I32), in_=words.rearrange("a p c -> p a c").bitcast(I32))

        def shift_scales(a, rows):
            nc.sync.dma_start(out=v_s0[a][0:rows, :].bitcast(I32), in_=v_s[P - rows : P, :].bitcast(I32))

        def gather_words(a, hf):
            nc.vector.tensor_copy(out=v_w[a][hf][:], in_=tab_w[a][:].indirect(offs_sb[:, 32 * hf : 32 * (hf + 1)]))

        def deal_w2(b):
            for copy, dealt, raw in (
                (nc.vector.tensor_copy, w2_s, w2_sraw[:, :, b * PASS : (b + 1) * PASS]),
                (nc.scalar.copy, w2_w, w2_raw[b][:]),
            ):
                copy(
                    out=dealt[b][:].rearrange("p a (i q) -> p a i q", i=PACK),
                    in_=raw.rearrange("p a (q i) -> p a i q", i=PACK),
                )

        load_table(0)
        load_w2(0)
        load_table(1)
        for q in range(4):
            nc.sync.dma_start(
                out=w2_sraw[32 * q : 32 * q + 4, :, :].bitcast(I32),
                in_=w2_scales[:, 4 * q : 4 * q + 4, :].rearrange("a r c -> r a c").bitcast(I32),
            )
        load_w1(0, 0)
        nc.vector.tensor_copy(out=v_s[:], in_=tab_s[:].indirect(offs_sb[:]))
        shift_scales(0, 104)
        load_w1(0, 1)
        shift_scales(1, 100)
        load_w2(1)
        nc.sync.dma_start(out=temp_sb[:], in_=temp.rearrange("(b p i) -> p b i", b=2, i=PACK))
        nc.sync.dma_start(pos1_sb[:], pos1)
        nc.sync.dma_start(pos2_sb[:], pos2)
        load_depth(0)
        load_w1(1, 0)
        load_w1(1, 1)
        load_depth(1)
        nc.sync.dma_start(out=w3_w[:].bitcast(I32), in_=w3_words.rearrange("a p c i -> p a (c i)").bitcast(I32))
        load_scales(nc.sync, w3_s, w3_scales, 0)
        nc.sync.dma_start(out=res_sb[:], in_=res.rearrange("(t p) m -> p t m", p=P))

        gather_words(0, 0)
        gather_words(0, 1)
        deal_w2(0)
        round_w1(nc.scalar.copy, 0, 0, 0)
        round_w1(nc.scalar.copy, 0, 0, 1)
        gather_words(1, 0)
        gather_words(1, 1)
        quantize_w1(0, 0, 0, 2)
        quantize_w1(0, 0, 2, PACK)
        round_w1(nc.vector.tensor_copy, 0, 1, 0)
        round_w1(nc.scalar.copy, 0, 1, 1)
        quantize_w1(0, 1, 0, 2)
        quantize_w1(0, 1, 2, PACK)
        nc.vector.tensor_scalar(neg_temp[:], temp_sb[:].rearrange("p b i -> p (b i)"), -1.0, None, ALU.mult)
        deal_w2(1)

        f_sb, h_sb = {}, {}

        def first_stage(t):
            b, i = divmod(t, PACK)
            cols = slice(i * P, (i + 1) * P)
            f_ps = [psum.tile([P, BANK], F32, name="f_bank") for hf in range(2)]
            g_ps = [psum.tile([P, BANK], F32, name="g_bank", bufs=2) for hf in range(2)]
            for hf in range(2):
                js = slice(hf * BANK, (hf + 1) * BANK)
                for a in range(2):
                    nc.tensor.matmul_mx(
                        out=f_ps[hf][:],
                        lhsT=w1_w[b][a][:, cols].bitcast(FP8X4),
                        lhsT_scale=w1_s[b][a][:, cols],
                        rhs=v_w[a][hf][:].bitcast(FP8X4),
                        rhs_scale=v_s0[0][4 * a : P, js],
                        start=(a == 0),
                        stop=(a == 1),
                    )
            for hf in range(2):
                js = slice(hf * BANK, (hf + 1) * BANK)
                for a in range(2):
                    nc.tensor.matmul_mx(
                        out=g_ps[hf][:],
                        lhsT=w2_w[b][:, a, cols].bitcast(FP4X4),
                        lhsT_scale=w2_s[b][:, a, cols],
                        rhs=v_w[a][hf][:].bitcast(FP8X4),
                        rhs_scale=v_s0[a][:, js],
                        start=(a == 0),
                        stop=(a == 1),
                    )
            tanh_f = ring.tile([P, S], F32, name="tanh_f", bufs=2)
            f_sb[t] = ring.tile([P, S], F32, name="f_sb")
            h_sb[t] = ring.tile([P, S], F32, name="h_sb")
            for hf in range(2):
                js = slice(hf * BANK, (hf + 1) * BANK)
                nc.scalar.activation(out=tanh_f[:, js], in_=f_ps[hf][:], func=ACT.Tanh)
                nc.vector.tensor_tensor(h_sb[t][:, js], g_ps[hf][:], tanh_f[:, js], ALU.add)
            return f_ps

        def keep_f(t, f_ps):
            for hf in range(2):
                nc.scalar.copy(out=f_sb[t][:, hf * BANK : (hf + 1) * BANK], in_=f_ps[hf][:])

        def row_bias(t):
            nc.vector.tensor_scalar(
                scaled[:], h_sb[t][:], neg_temp[:, t : t + 1], None, ALU.mult, ALU.min, accum_out=bias[:, t : t + 1]
            )

        def pick_f(t, parts, factor):
            b, i = divmod(t, PACK)
            width = M // parts
            for u in range(parts):
                ms = slice(u * width, (u + 1) * width)
                picked = f_sb[t][:].indirect(pos2_sb[:, u * width // 16 : (u + 1) * width // 16])
                nc.vector.tensor_tensor(pick[b][:, i, ms], picked, factor[b][:, i, ms], ALU.mult)

        def look_h(t, parts):
            b, i = divmod(t, PACK)
            width = M // parts
            for u in range(parts):
                nc.scalar.activation(
                    out=look[b][:, i, u * width : (u + 1) * width],
                    in_=h_sb[t][:].indirect(pos1_sb[:, u * width // 16 : (u + 1) * width // 16]),
                    func=ACT.Exp,
                    bias=bias[:, t : t + 1],
                    scale=temp_sb[:, b, i : i + 1],
                )

        def make_y(t):
            b, i = divmod(t, PACK)
            for u in range(M // 256):
                ms = slice(u * 256, (u + 1) * 256)
                nc.gpsimd.tensor_tensor(y_two[b][:, i // 2, ms, i % 2], pick[b][:, i, ms], look[b][:, i, ms], ALU.mult)

        def make_last_y(hf):
            ms = slice(hf * 256, (hf + 1) * 256)
            nc.vector.tensor_tensor(
                y_two[1][:, 1, ms, :].rearrange("p (c u) i -> p c i u", u=4),
                pick[1][:, 2:4, ms].rearrange("p i (c u) -> p c i u", u=4),
                look[1][:, 2:4, ms].rearrange("p i (c u) -> p c i u", u=4),
                ALU.mult,
            )

        def quantize_y(b, ms):
            nc.scalar.copy(
                out=y_bf[b][:, ms, :].rearrange("p m i -> p (m i)").bitcast(F32).rearrange("p (m u) -> p m u", u=2),
                in_=y_two[b][:, :, ms, :].rearrange("p u m l -> p u (m l)").bitcast(F32).rearrange("p u m -> p m u"),
            )
            quantize(y_w[b][:, ms], y_s[b][:, ms], y_bf[b][:, ms, :].rearrange("p m i -> p (m i)"))

        tiles = 2 * PACK
        rounders = (nc.vector.tensor_copy, nc.scalar.copy, nc.scalar.copy, nc.scalar.copy)
        for t in range(tiles):
            f_ps = first_stage(t)
            if t > 0:
                look_h(t - 1, 1)
                pick_f(t - 1, 1, dep)
                if t < tiles - 1:
                    make_y(t - 1)
            keep_f(t, f_ps)
            row_bias(t)
            for n in {0:(0,),1:(1,),2:(2,3,)}.get(t, ()):
                a, c = divmod(n, 2)
                round_w1(rounders[n], 1, a, c)
                if c == 1:
                    quantize_w1(1, a)
            if t == 5:
                quantize_y(0, slice(0, M))
        pick_f(tiles - 1, 2, dep)
        look_h(tiles - 1, 2)

        out_v = out.rearrange("(t p) m -> p t m", p=P)
        acc = {}
        for hf in range(2):
            for k in range(2):
                acc[hf, k] = psum.tile([P, 2, 256], F32, name=("acc_bank", "f_bank")[hf], bufs=(2, 4)[hf])

        def second_stage(b, hf):
            for k in range(2):
                for u in range(2):
                    ns = slice((2 * k + u) * P, (2 * k + u + 1) * P)
                    nc.tensor.matmul_mx(
                        out=acc[hf, k][:, u, :],
                        lhsT=w3_w[:, b, ns].bitcast(FP8X4),
                        lhsT_scale=w3_s[4 * b : P, ns],
                        rhs=y_w[b][:, hf * 256 : (hf + 1) * 256].bitcast(FP8X4),
                        rhs_scale=y_s[b][:, hf * 256 : (hf + 1) * 256],
                        start=(b == 0 and u == 0),
                        stop=(b == 1 and u == 1),
                    )

        for hf in range(2):
            second_stage(0, hf)
        for hf in range(2):
            make_last_y(hf)
            quantize_y(1, slice(hf * 256, (hf + 1) * 256))
            second_stage(1, hf)
        for hf in range(2):
            ms = slice(hf * 256, (hf + 1) * 256)
            for k in range(2):
                parts = 2 if (hf, k) == (1, 1) else 1
                for u in range(parts):
                    us = slice(u * 2 // parts, (u + 1) * 2 // parts)
                    ns = slice(2 * k + us.start, 2 * k + us.stop)
                    total = ring.tile([P, 2 // parts, 256], F32, name="total")
                    score = ring.tile([P, 2 // parts, 256], F32, name="score", bufs=5)
                    nc.vector.tensor_tensor(total[:], acc[hf, k][:, us, :], res_sb[:, ns, ms], ALU.add)
                    nc.scalar.activation(out=score[:], in_=total[:], func=ACT.Tanh)
                    nc.sync.dma_start(out=out_v[:, ns, ms], in_=score[:])
